import numpy as np
import ml_dtypes


def mxq(x, axis, fmt="e4m3"):
    dtype, down = {"e4m3": (ml_dtypes.float8_e4m3fn, 7), "e5m2": (ml_dtypes.float8_e5m2, 14)}[fmt]
    v = np.moveaxis(np.asarray(x, np.float32).astype(ml_dtypes.bfloat16).astype(np.float64), axis, -1)
    blocks = v.reshape(v.shape[:-1] + (-1, 32))
    amax = np.abs(blocks).max(-1, keepdims=True)
    byte = np.maximum(np.where(amax > 0, np.frexp(amax)[1] - 1 + 127, 0) - down, 1)
    scale = np.exp2(byte - 127.0)
    codes = (blocks / scale).astype(np.float32).astype(dtype).astype(np.float64)
    return np.moveaxis((codes * scale).reshape(v.shape), -1, axis)


WIDE = False


def mx_kscale(k):
    if not WIDE:
        return np.ones(k)
    levels = np.array([10, -10, 5, -5, 0])
    if k % 512:
        return np.exp2(np.random.permutation(np.resize(levels, k // 32))).repeat(32)
    a = np.empty((k // 512, 16))
    for p in range(k // 512):
        a[p, :8] = np.random.permutation(np.resize(levels, 8))
        for g in range(8):
            far = levels[np.abs(levels - a[p, g]) >= 10]
            a[p, g + 8] = far[np.random.randint(len(far))]
    return np.exp2(a.ravel()).repeat(32)


def f64(x):
    return np.asarray(x).astype(np.float64)


def striped(idx):
    return np.tile(np.asarray(idx).reshape(-1, 16).T, (8, 1)).astype(np.uint16)


def unstriped(offs):
    return offs[:16].T.reshape(-1).astype(np.int64)


E2M1 = np.array([0.0, 0.5, 1.0, 1.5, 2.0, 3.0, 4.0, 6.0, -0.0, -0.5, -1.0, -1.5, -2.0, -3.0, -4.0, -6.0])


def pack_weight(w, fmt):
    k, n = w.shape
    w = f64(np.asarray(w, np.float32).astype(ml_dtypes.bfloat16)).reshape(k // 32, 32, n)
    amax = np.abs(w).max(1)
    if fmt == "e4m3":
        byte = np.frexp(amax)[1] - 1 + 127 - 7
    else:
        mant, ex = np.frexp(amax / 6.0)
        byte = np.where(mant > 0.5, ex, ex - 1) + 127
    byte = np.clip(np.where(amax > 0, byte, 1), 1, 254)
    scaled = (w * np.exp2(127.0 - byte)[:, None, :]).reshape(k, n).astype(np.float32)
    by_word = np.ascontiguousarray(scaled.reshape(k // 512, 128, 4, n).transpose(0, 1, 3, 2))
    if fmt == "e4m3":
        words = by_word.astype(ml_dtypes.float8_e4m3fn).view(np.uint8)
    else:
        c = by_word.astype(ml_dtypes.float4_e2m1fn).view(np.uint8) & 0xF
        words = (c[..., 0::2] | (c[..., 1::2] << 4)).reshape(k // 512, 128, 2 * n)
    return np.ascontiguousarray(words), np.ascontiguousarray(byte.astype(np.uint8).reshape(k // 512, 16, n))


def unpack_weight(words, scales, fmt):
    g, _, n = scales.shape
    words = np.ascontiguousarray(words).reshape(g, 128, n, -1)
    if fmt == "e4m3":
        vals = words.view(ml_dtypes.float8_e4m3fn).astype(np.float64)
    else:
        nib = np.empty((g, 128, n, 4), np.uint8)
        nib[..., 0::2] = words & 0xF
        nib[..., 1::2] = words >> 4
        vals = E2M1[nib]
    vals = vals * np.repeat(np.exp2(scales.astype(np.float64) - 127.0), 8, axis=1)[..., None]
    return vals.transpose(0, 1, 3, 2).reshape(g * 512, n)


D, T, U, I, G, Q, E = 512, 2048, 512, 1024, 64, 128, 512


def setup_inputs():
    n = np.random.standard_normal
    idx = (np.random.permutation(T // 16)[:I // 16, None] * 16 + np.arange(16)).reshape(-1)
    idx2 = np.random.permutation(U)[:G]
    fd = mx_kscale(D)
    fi = mx_kscale(I)
    keysp = pack_weight(n((D, T)) / fd[:, None], "e4m3")
    marksp = pack_weight(n((D, U)) / fd[:, None], "e4m3")
    return {
        "query": (n((D, Q)) * 0.4 / np.sqrt(D) * fd[:, None]).astype(np.float32),
        "keys_words": keysp[0],
        "keys_scales": keysp[1],
        "marks_words": marksp[0],
        "marks_scales": marksp[1],
        "fac": (np.random.uniform(0.5, 2.0, (1, I)) * fi).astype(np.float32),
        "vals": (n((I, E)) / fi[:, None]).astype(np.float32),
        "offs": striped(idx),
        "offs2": striped(idx2),
    }


def reference(query, keys_words, keys_scales, marks_words, marks_scales, fac, vals, offs, offs2):
    idx = unstriped(offs)
    idx2 = unstriped(offs2)
    keysu = unpack_weight(keys_words, keys_scales, "e4m3")
    marksu = unpack_weight(marks_words, marks_scales, "e4m3")
    queryq = mxq(f64(query), 0, "e4m3")
    keysidxg = keysu[:, idx]
    a = queryq.T @ keysidxg
    marksidx2g = marksu[:, idx2]
    b = queryq.T @ marksidx2g
    p = np.exp(a)
    z = p.reshape(Q, G, I // G).sum(axis=2)
    r = np.exp(b - np.max(b, axis=1, keepdims=True))
    s = r / np.sum(r, axis=1, keepdims=True) / z
    sr = np.repeat(s, I // G, axis=1)
    w = p * sr * f64(fac)
    wt = w.T
    wtq = mxq(wt, 0, "e4m3")
    valsq = mxq(f64(vals), 0, "e4m3")
    o = wtq.T @ valsq
    return o

@@ -1,0 +1,210 @@
+from contextlib import ExitStack
+
+import concourse.mybir as mybir
+from concourse.masks import make_identity
+
+D, T, U, I, G, Q, E = 512, 2048, 512, 1024, 64, 128, 512
+FLOPS = 2 * D * Q * (I + G) + 2 * I * Q * E
+
+F32 = mybir.dt.float32
+BF16 = mybir.dt.bfloat16
+I32 = mybir.dt.int32
+U32 = mybir.dt.uint32
+U16 = mybir.dt.uint16
+U8 = mybir.dt.uint8
+FP8X4 = mybir.dt.float8_e4m3fn_x4
+ALU = mybir.AluOpType
+ACT = mybir.ActivationFunctionType
+AXIS = mybir.AxisListType
+
+P = 128
+PACK = 4
+K_PASS = P * PACK
+PASSES = I // K_PASS
+PAGE = I // G
+PAGES = K_PASS // PAGE
+HALF = E // 2
+
+
+def load_scale_rows(queue, plane, rows):
+    for quad in range(4):
+        queue.dma_start(plane[32 * quad : 32 * quad + 4, :].bitcast(I32), rows[0, 4 * quad : 4 * quad + 4, :].bitcast(I32))
+
+
+def interleave_views(grouped, raw):
+    return (
+        grouped.rearrange("p (c i) t -> p c t i", i=4),
+        raw.rearrange("p t (c i) -> p c t i", i=4),
+    )
+
+
+def tile_attend_landmark_kernel(tc, query, keys_words, keys_scales, marks_words, marks_scales, fac, vals, offs, offs2, out):
+    nc = tc.nc
+    with ExitStack() as ctx:
+        lists = ctx.enter_context(tc.tile_pool(name="lists", bufs=1))
+        sb = ctx.enter_context(tc.tile_pool(name="sb", bufs=1))
+        psum = ctx.enter_context(tc.psum_pool(name="psum", bufs=1))
+
+        key_list = lists.tile([P, I // 16], U16, name="key_list")
+        mark_list = lists.tile([P, G // 16], U16, name="mark_list")
+
+        key_plane = sb.tile([P, T], U8, name="key_plane", align_bytes=64)
+        mark_plane = sb.tile([P, U], U8, name="mark_plane", align_bytes=64)
+        key_pool = sb.tile([P, T], I32, name="key_pool", align_bytes=64)
+        mark_pool = sb.tile([P, U], I32, name="mark_pool", align_bytes=64)
+        q_raw = sb.tile([P, PACK, Q], F32, name="q_raw", align_bytes=64)
+        fac_t = sb.tile([P, PASSES, PACK], F32, name="fac_t", tag="fac_t", align_bytes=64)
+        ident = sb.tile([P, P], F32, name="ident", align_bytes=64)
+
+        nc.gpsimd.memset(key_plane[:].bitcast(I32), 0)
+        nc.gpsimd.memset(mark_plane[:].bitcast(I32), 0)
+        nc.gpsimd.dma_start(fac_t[:], fac.rearrange("o (h p j) -> p (o h) j", p=P, j=PACK))
+        make_identity(nc, ident[:])
+
+        warm_in = sb.tile([P, 1], F32, name="warm_in")
+        warm_out = sb.tile([P, 1], F32, name="warm_out")
+        nc.gpsimd.memset(warm_in[:], 0.0)
+        nc.scalar.activation(warm_out[:], warm_in[:], ACT.Exp)
+
+        v_rows = vals.rearrange("(h p j) e -> h p j e", p=P, j=PACK)
+        v_raw = {}
+
+        def load_vals(h, u):
+            v_raw[h, u] = sb.tile([P, PACK, HALF], F32, name="v_raw%d_%d" % (h, u), tag="v_raw%d_%d" % (h, u), align_bytes=64)
+            nc.sync.dma_start(v_raw[h, u][:], v_rows[h][:, :, u * HALF : (u + 1) * HALF])
+
+        load_scale_rows(nc.sync, key_plane, keys_scales)
+        nc.sync.dma_start(key_list[:], offs)
+        nc.sync.dma_start(q_raw[:], query.rearrange("(p j) q -> p j q", j=PACK))
+        nc.sync.dma_start(key_pool[:], keys_words[0].rearrange("p n t -> p (n t)").bitcast(I32))
+        load_vals(0, 0)
+        load_vals(0, 1)
+        nc.sync.dma_start(mark_list[:], offs2)
+        load_scale_rows(nc.sync, mark_plane, marks_scales)
+        nc.sync.dma_start(mark_pool[:], marks_words[0].rearrange("p n t -> p (n t)").bitcast(I32))
+        load_vals(1, 0)
+        load_vals(1, 1)
+
+        q_bf = sb.tile([P, Q, PACK], BF16, name="q_bf", align_bytes=64)
+        q_codes = sb.tile([P, Q], U32, name="q_codes", align_bytes=64)
+        q_plane = sb.tile([P, Q], U8, name="q_plane", align_bytes=64)
+        dst, src = interleave_views(q_bf[:], q_raw[:])
+        nc.scalar.copy(dst, src)
+
+        k_plane = sb.tile([P, I], U8, name="k_plane", align_bytes=64)
+        nc.vector.tensor_copy(k_plane[:], key_plane[:].indirect(key_list[:]))
+        nc.vector.quantize_mx(out=q_codes[:].bitcast(FP8X4), scales=q_plane[:], in_=q_bf[:].rearrange("p q t -> p (q t)"))
+        scores = []
+        for h in range(PASSES):
+            k_codes = sb.tile([P, K_PASS], U32, name="k_codes%d" % h, align_bytes=64)
+            cols = slice(h * K_PASS // 16, (h + 1) * K_PASS // 16)
+            nc.vector.tensor_copy(k_codes[:], key_pool[:].bitcast(U32).indirect(key_list[:, cols]))
+            a = psum.tile([P, K_PASS], F32, name="a%d" % h, tag="bank%d" % h)
+            nc.tensor.matmul_mx(
+                out=a[:], lhsT=q_codes[:].bitcast(FP8X4), lhsT_scale=q_plane[:],
+                rhs=k_codes[:].bitcast(FP8X4), rhs_scale=k_plane[:, h * K_PASS : (h + 1) * K_PASS],
+                start=True, stop=True,
+            )
+            scores.append(a)
+        m_plane = sb.tile([P, G], U8, name="m_plane", align_bytes=64)
+        m_codes = sb.tile([P, G], U32, name="m_codes", align_bytes=64)
+        nc.vector.tensor_copy(m_plane[:], mark_plane[:].indirect(mark_list[:]))
+        nc.vector.tensor_copy(m_codes[:], mark_pool[:].bitcast(U32).indirect(mark_list[:]))
+        b = psum.tile([P, G], F32, name="b", tag="bank2")
+        nc.tensor.matmul_mx(
+            out=b[:], lhsT=q_codes[:].bitcast(FP8X4), lhsT_scale=q_plane[:],
+            rhs=m_codes[:].bitcast(FP8X4), rhs_scale=m_plane[:], start=True, stop=True,
+        )
+
+        neg_max = sb.tile([P, 1], F32, name="neg_max")
+        r = sb.tile([P, G], F32, name="r")
+        r_sum = sb.tile([P, 1], F32, name="r_sum")
+        r_inv = sb.tile([P, 1], F32, name="r_inv")
+
+        v_bfs = {}
+
+        def cast_vals(h, u):
+            tag = "fac_t" if (h, u) == (1, 1) else "v_bf%d_%d" % (h, u)
+            v_bfs[h, u] = sb.tile([P, HALF, PACK], BF16, name="v_bf%d_%d" % (h, u), tag=tag, align_bytes=64)
+            dst, src = interleave_views(v_bfs[h, u][:], v_raw[h, u][:])
+            nc.scalar.copy(dst, src)
+
+        cast_vals(0, 0)
+        cast_vals(0, 1)
+        p_all = sb.tile([P, PASSES, PACK, P], F32, name="p_all", tag="v_raw0_1", align_bytes=64)
+        p_tiles = []
+        for h in range(PASSES):
+            p = p_all[:, h]
+            nc.scalar.activation(p, scores[h][:].rearrange("q (s t) -> q t s", t=PACK), ACT.Exp)
+            p_tiles.append(p)
+        nc.vector.tensor_reduce(neg_max[:], b[:], AXIS.X, ALU.max, negate=True)
+        nc.scalar.activation(r[:], b[:], ACT.Exp, bias=neg_max[:], accum_out=r_sum[:])
+
+        z_tiles, pf_tiles = [], []
+        for h in range(PASSES):
+            p = p_tiles[h]
+            z = sb.tile([P, PAGES], F32, name="z%d" % h)
+            nc.vector.tensor_reduce(z[:], p.rearrange("q t (g j) -> q g t j", j=PACK), AXIS.XY, ALU.add)
+            z_tiles.append(z)
+            p_turned = psum.tile([P, PACK, Q], F32, name="p_turned%d" % h, tag="bank%d" % (3 + h))
+            for t in range(PACK):
+                nc.tensor.transpose(p_turned[:, t, :], p[:, t, :], ident[:])
+            pf = sb.tile([P, PACK, Q], F32, name="pf%d" % h, align_bytes=64)
+            for t in range(PACK):
+                nc.scalar.activation(pf[:, t, :], p_turned[:, t, :], ACT.Copy, scale=fac_t[:, h, t : t + 1])
+            pf_tiles.append(pf)
+        nc.vector.reciprocal(r_inv[:], r_sum[:])
+        z_invs = []
+        for h in range(PASSES):
+            z_inv = sb.tile([P, PAGES], F32, name="z_inv%d" % h)
+            nc.vector.reciprocal(z_inv[:], z_tiles[h][:])
+            z_invs.append(z_inv)
+        shares = []
+        for h in range(PASSES):
+            share = sb.tile([P, PAGES, PACK], F32, name="share%d" % h, align_bytes=64)
+            nc.vector.scalar_tensor_tensor(
+                share[:], z_invs[h][:].unsqueeze(2).to_broadcast([P, PAGES, PACK]), r_inv[:],
+                r[:, h * PAGES : (h + 1) * PAGES].unsqueeze(2).to_broadcast([P, PAGES, PACK]), ALU.mult, ALU.mult,
+            )
+            share_turned = psum.tile([P, Q], F32, name="share_turned%d" % h, tag="bank%d" % (5 + h))
+            nc.tensor.transpose(share_turned[:], share[:].rearrange("q g j -> q (g j)"), ident[:])
+            shares.append(share_turned)
+        w_bfs = []
+        for h in range(PASSES):
+            w_bf = sb.tile([P, Q, PACK], BF16, name="w_bf%d" % h, align_bytes=64)
+            dst, src = interleave_views(w_bf[:], pf_tiles[h][:])
+            nc.vector.tensor_tensor(
+                dst, src,
+                shares[h][:].rearrange("s (c i) -> s c i", i=4).unsqueeze(2).to_broadcast([P, Q // 4, PACK, 4]),
+                ALU.mult,
+            )
+            w_bfs.append(w_bf)
+        w_codes, w_planes = [], []
+        for h in range(PASSES):
+            w_codes.append(sb.tile([P, Q], U32, name="w_codes%d" % h, align_bytes=64))
+            w_planes.append(sb.tile([P, Q], U8, name="w_plane%d" % h, align_bytes=64))
+            nc.vector.quantize_mx(out=w_codes[h][:].bitcast(FP8X4), scales=w_planes[h][:], in_=w_bfs[h][:].rearrange("p q t -> p (q t)"))
+
+        acc = [psum.tile([P, HALF], F32, name="acc%d" % u, tag="bank%d" % u) for u in range(2)]
+        for h in range(PASSES):
+            for u in range(2):
+                if (h, u) not in v_bfs:
+                    cast_vals(h, u)
+                v_bf = v_bfs[h, u]
+                v_codes = sb.tile([P, HALF], U32, name="v_codes%d_%d" % (h, u), align_bytes=64)
+                v_plane = sb.tile([P, HALF], U8, name="v_plane%d_%d" % (h, u), align_bytes=64)
+                nc.vector.quantize_mx(out=v_codes[:].bitcast(FP8X4), scales=v_plane[:], in_=v_bf[:].rearrange("p e t -> p (e t)"))
+                nc.tensor.matmul_mx(
+                    out=acc[u][:], lhsT=w_codes[h][:].bitcast(FP8X4), lhsT_scale=w_planes[h][:],
+                    rhs=v_codes[:].bitcast(FP8X4), rhs_scale=v_plane[:],
+                    start=(h == 0), stop=(h == PASSES - 1),
+                )
+
+        for u in range(2):
+            result = sb.tile([P, HALF], F32, name="result%d" % u)
+            if u == 0:
+                nc.scalar.copy(result[:], acc[u][:])
+                nc.scalar.dma_start(out[:, u * HALF : (u + 1) * HALF], result[:])
+            else:
+                nc.vector.tensor_copy(result[:], acc[u][:])
+                nc.sync.dma_start(out[:, u * HALF : (u + 1) * HALF], result[:])

@@ -22,19 +22,41 @@ PACK = 4
 K_PASS = P * PACK
 PASSES = I // K_PASS
 PAGE = I // G
-PAGES = K_PASS // PAGE
+PAGES = G // PASSES
+LIST_ROWS = 16
 HALF = E // 2
+RUN = 4
+BANK = 2048
+CHUNKS = [(0, K_PASS), (K_PASS, K_PASS // 2), (K_PASS + K_PASS // 2, K_PASS // 2)]
+SCORE_BANKS = [0, 1, 6]
+ALIGN = 64
 
 
-def load_scale_rows(queue, plane, rows):
-    for quad in range(4):
-        queue.dma_start(plane[32 * quad : 32 * quad + 4, :].bitcast(I32), rows[0, 4 * quad : 4 * quad + 4, :].bitcast(I32))
+def load_scale_rows(nc, plane, rows):
+    for n in range(4):
+        nc.sync.dma_start(plane[32 * n : 32 * n + 4, :].bitcast(I32), rows[0, 4 * n : 4 * n + 4, :].bitcast(I32))
 
 
-def interleave_views(grouped, raw):
+def interleave_views(grouped, rows):
     return (
-        grouped.rearrange("p (c i) t -> p c t i", i=4),
-        raw.rearrange("p t (c i) -> p c t i", i=4),
+        grouped.rearrange("p (c i) t -> p c t i", i=RUN),
+        rows.rearrange("p t (c i) -> p c t i", i=RUN),
+    )
+
+
+def quantise(nc, codes, plane, grouped):
+    nc.vector.quantize_mx(out=codes.bitcast(FP8X4), scales=plane, in_=grouped.rearrange("p c t -> p (c t)"))
+
+
+def product(nc, out, stationary, moving, start=True, stop=True):
+    nc.tensor.matmul_mx(
+        out=out,
+        lhsT=stationary[0].bitcast(FP8X4),
+        lhsT_scale=stationary[1],
+        rhs=moving[0].bitcast(FP8X4),
+        rhs_scale=moving[1],
+        start=start,
+        stop=stop,
     )
 
 
@@ -43,168 +65,167 @@ def tile_attend_landmark_kernel(tc, query, keys_words, keys_scales, marks_words,
     with ExitStack() as ctx:
         lists = ctx.enter_context(tc.tile_pool(name="lists", bufs=1))
         sb = ctx.enter_context(tc.tile_pool(name="sb", bufs=1))
+        reused = ctx.enter_context(tc.tile_pool(name="reused", bufs=1))
         psum = ctx.enter_context(tc.psum_pool(name="psum", bufs=1))
 
-        key_list = lists.tile([P, I // 16], U16, name="key_list")
-        mark_list = lists.tile([P, G // 16], U16, name="mark_list")
+        p_bytes = K_PASS * 4
+        marks_at = PASSES * p_bytes
+        sums_bytes = 3 * ALIGN
 
-        key_plane = sb.tile([P, T], U8, name="key_plane", align_bytes=64)
-        mark_plane = sb.tile([P, U], U8, name="mark_plane", align_bytes=64)
-        key_pool = sb.tile([P, T], I32, name="key_pool", align_bytes=64)
-        mark_pool = sb.tile([P, U], I32, name="mark_pool", align_bytes=64)
-        q_raw = sb.tile([P, PACK, Q], F32, name="q_raw", align_bytes=64)
-        fac_t = sb.tile([P, PASSES, PACK], F32, name="fac_t", tag="fac_t", align_bytes=64)
-        ident = sb.tile([P, P], F32, name="ident", align_bytes=64)
+        key_list = lists.tile([P, I // LIST_ROWS], U16, name="key_list")
+        mark_list = lists.tile([P, G // LIST_ROWS], U16, name="mark_list")
+        key_plane = sb.tile([P, T], U8, name="key_plane", align_bytes=ALIGN)
+        mark_plane = sb.tile([P, U], U8, name="mark_plane", align_bytes=ALIGN)
+        key_pool = sb.tile([P, T], I32, name="key_pool", align_bytes=ALIGN)
+        mark_pool = reused.tile([P, U], I32, name="mark_pool", offset=marks_at, align_bytes=ALIGN)
+        q_raw = sb.tile([P, PACK, Q], F32, name="q_raw", align_bytes=ALIGN)
+        fac_t = sb.tile([P, PASSES, PACK], F32, name="fac_t", tag="fac_t", align_bytes=ALIGN)
+        ident = sb.tile([P, P], F32, name="ident", align_bytes=ALIGN)
 
         nc.gpsimd.memset(key_plane[:].bitcast(I32), 0)
         nc.gpsimd.memset(mark_plane[:].bitcast(I32), 0)
-        nc.gpsimd.dma_start(fac_t[:], fac.rearrange("o (h p j) -> p (o h) j", p=P, j=PACK))
-        make_identity(nc, ident[:])
-
         warm_in = sb.tile([P, 1], F32, name="warm_in")
         warm_out = sb.tile([P, 1], F32, name="warm_out")
         nc.gpsimd.memset(warm_in[:], 0.0)
         nc.scalar.activation(warm_out[:], warm_in[:], ACT.Exp)
+        make_identity(nc, ident[:])
 
-        v_rows = vals.rearrange("(h p j) e -> h p j e", p=P, j=PACK)
-        v_raw = {}
+        v_rows = vals.rearrange("(h p t) e -> h p t e", p=P, t=PACK)
+        v_raw = {
+            (0, 0): reused.tile([P, PACK, HALF], F32, name="v_raw0_0", offset=0, align_bytes=ALIGN),
+            (0, 1): sb.tile([P, PACK, HALF], F32, name="v_raw0_1", align_bytes=ALIGN),
+            (1, 0): sb.tile([P, PACK, HALF], F32, name="v_raw1_0", align_bytes=ALIGN),
+            (1, 1): sb.tile([P, PACK, HALF], F32, name="v_raw1_1", align_bytes=ALIGN),
+        }
 
-        def load_vals(h, u):
-            v_raw[h, u] = sb.tile([P, PACK, HALF], F32, name="v_raw%d_%d" % (h, u), tag="v_raw%d_%d" % (h, u), align_bytes=64)
+        def load_values(h, u):
             nc.sync.dma_start(v_raw[h, u][:], v_rows[h][:, :, u * HALF : (u + 1) * HALF])
 
-        load_scale_rows(nc.sync, key_plane, keys_scales)
+        load_scale_rows(nc, key_plane, keys_scales)
         nc.sync.dma_start(key_list[:], offs)
-        nc.sync.dma_start(q_raw[:], query.rearrange("(p j) q -> p j q", j=PACK))
-        nc.sync.dma_start(key_pool[:], keys_words[0].rearrange("p n t -> p (n t)").bitcast(I32))
-        load_vals(0, 0)
-        load_vals(0, 1)
         nc.sync.dma_start(mark_list[:], offs2)
-        load_scale_rows(nc.sync, mark_plane, marks_scales)
+        nc.sync.dma_start(q_raw[:], query.rearrange("(p t) q -> p t q", t=PACK))
+        nc.sync.dma_start(key_pool[:], keys_words[0].rearrange("p n t -> p (n t)").bitcast(I32))
+        load_values(0, 0)
+        load_values(0, 1)
+        load_scale_rows(nc, mark_plane, marks_scales)
         nc.sync.dma_start(mark_pool[:], marks_words[0].rearrange("p n t -> p (n t)").bitcast(I32))
-        load_vals(1, 0)
-        load_vals(1, 1)
+        load_values(1, 0)
+        nc.sync.dma_start(fac_t[:], fac.rearrange("o (h p t) -> p (o h) t", p=P, t=PACK))
+        load_values(1, 1)
 
-        q_bf = sb.tile([P, Q, PACK], BF16, name="q_bf", align_bytes=64)
-        q_codes = sb.tile([P, Q], U32, name="q_codes", align_bytes=64)
-        q_plane = sb.tile([P, Q], U8, name="q_plane", align_bytes=64)
-        dst, src = interleave_views(q_bf[:], q_raw[:])
-        nc.scalar.copy(dst, src)
-
-        k_plane = sb.tile([P, I], U8, name="k_plane", align_bytes=64)
+        q_bf = sb.tile([P, Q, PACK], BF16, name="q_bf", align_bytes=ALIGN)
+        q_codes = sb.tile([P, Q], U32, name="q_codes", align_bytes=ALIGN)
+        q_plane = sb.tile([P, Q], U8, name="q_plane", align_bytes=ALIGN)
+        nc.scalar.copy(*interleave_views(q_bf[:], q_raw[:]))
+        k_plane = sb.tile([P, I], U8, name="k_plane", align_bytes=ALIGN)
         nc.vector.tensor_copy(k_plane[:], key_plane[:].indirect(key_list[:]))
-        nc.vector.quantize_mx(out=q_codes[:].bitcast(FP8X4), scales=q_plane[:], in_=q_bf[:].rearrange("p q t -> p (q t)"))
+        quantise(nc, q_codes[:], q_plane[:], q_bf[:])
+        queries = (q_codes[:], q_plane[:])
         scores = []
-        for h in range(PASSES):
-            k_codes = sb.tile([P, K_PASS], U32, name="k_codes%d" % h, align_bytes=64)
-            cols = slice(h * K_PASS // 16, (h + 1) * K_PASS // 16)
-            nc.vector.tensor_copy(k_codes[:], key_pool[:].bitcast(U32).indirect(key_list[:, cols]))
-            a = psum.tile([P, K_PASS], F32, name="a%d" % h, tag="bank%d" % h)
-            nc.tensor.matmul_mx(
-                out=a[:], lhsT=q_codes[:].bitcast(FP8X4), lhsT_scale=q_plane[:],
-                rhs=k_codes[:].bitcast(FP8X4), rhs_scale=k_plane[:, h * K_PASS : (h + 1) * K_PASS],
-                start=True, stop=True,
-            )
-            scores.append(a)
-        m_plane = sb.tile([P, G], U8, name="m_plane", align_bytes=64)
-        m_codes = sb.tile([P, G], U32, name="m_codes", align_bytes=64)
+        for n, (first, width) in enumerate(CHUNKS):
+            entries = key_list[:, first // LIST_ROWS : (first + width) // LIST_ROWS]
+            k_codes = sb.tile([P, width], U32, name="k_codes%d" % n, align_bytes=ALIGN)
+            nc.vector.tensor_copy(k_codes[:], key_pool[:].bitcast(U32).indirect(entries))
+            scores.append(psum.tile([P, width], F32, name="scores%d" % n, offset=SCORE_BANKS[n] * BANK))
+            product(nc, scores[n][:], queries, (k_codes[:], k_plane[:, first : first + width]))
+
+        m_plane = sb.tile([P, G], U8, name="m_plane", align_bytes=ALIGN)
+        m_codes = sb.tile([P, G], U32, name="m_codes", align_bytes=ALIGN)
         nc.vector.tensor_copy(m_plane[:], mark_plane[:].indirect(mark_list[:]))
         nc.vector.tensor_copy(m_codes[:], mark_pool[:].bitcast(U32).indirect(mark_list[:]))
-        b = psum.tile([P, G], F32, name="b", tag="bank2")
-        nc.tensor.matmul_mx(
-            out=b[:], lhsT=q_codes[:].bitcast(FP8X4), lhsT_scale=q_plane[:],
-            rhs=m_codes[:].bitcast(FP8X4), rhs_scale=m_plane[:], start=True, stop=True,
-        )
+        mark_banks = psum.tile([P, PASSES * K_PASS], F32, name="mark_banks", offset=2 * BANK)
+        mark_scores = mark_banks[:, 0:G]
+        product(nc, mark_scores, queries, (m_codes[:], m_plane[:]))
 
-        neg_max = sb.tile([P, 1], F32, name="neg_max")
+        neg_max = sb.tile([P, 1], F32, name="neg_max", tag="neg_max", align_bytes=ALIGN)
+        v_bf = {}
+        values = {}
+
+        def round_values(h, u, tag):
+            v_bf[h, u] = sb.tile([P, HALF, PACK], BF16, name="v_bf%d_%d" % (h, u), tag=tag, align_bytes=ALIGN)
+            nc.scalar.copy(*interleave_views(v_bf[h, u][:], v_raw[h, u][:]))
+
+        def quantise_values(h, u, codes):
+            plane = sb.tile([P, HALF], U8, name="v_plane%d_%d" % (h, u), align_bytes=ALIGN)
+            quantise(nc, codes[:], plane[:], v_bf[h, u][:])
+            values[h, u] = (codes[:], plane[:])
+
+        round_values(0, 0, "v_bf0_0")
+        quantise_values(0, 0, sb.tile([P, HALF], U32, name="codes0_0", align_bytes=ALIGN))
+        v_bf[0, 1] = reused.tile([P, HALF, PACK], BF16, name="v_bf0_1", offset=marks_at + PASSES * sums_bytes, align_bytes=ALIGN)
+        nc.gpsimd.tensor_scalar(v_bf[0, 1][:], v_raw[0, 1][:].rearrange("p t e -> p e t"), 1.0, 0.0, ALU.mult, ALU.add)
+
+        p = [reused.tile([P, PACK, P], F32, name="p%d" % h, offset=h * p_bytes, align_bytes=ALIGN) for h in range(PASSES)]
+        for n, (first, width) in enumerate(CHUNKS):
+            h, s0 = first // K_PASS, first % K_PASS // PACK
+            nc.scalar.activation(p[h][:, :, s0 : s0 + width // PACK], scores[n][:].rearrange("q (s t) -> q t s", t=PACK), ACT.Exp)
+        sum_width = [PAGES + 1, PAGES]
+        sums = [
+            reused.tile([P, sum_width[h]], F32, name="sums%d" % h, offset=marks_at + h * sums_bytes, align_bytes=ALIGN)
+            for h in range(PASSES)
+        ]
         r = sb.tile([P, G], F32, name="r")
-        r_sum = sb.tile([P, 1], F32, name="r_sum")
-        r_inv = sb.tile([P, 1], F32, name="r_inv")
+        nc.vector.tensor_reduce(neg_max[:], mark_scores, AXIS.X, ALU.max, negate=True)
+        nc.scalar.activation(r[:], mark_scores, ACT.Exp, bias=neg_max[:], accum_out=sums[0][:, PAGES : PAGES + 1])
 
-        v_bfs = {}
-
-        def cast_vals(h, u):
-            tag = "fac_t" if (h, u) == (1, 1) else "v_bf%d_%d" % (h, u)
-            v_bfs[h, u] = sb.tile([P, HALF, PACK], BF16, name="v_bf%d_%d" % (h, u), tag=tag, align_bytes=64)
-            dst, src = interleave_views(v_bfs[h, u][:], v_raw[h, u][:])
-            nc.scalar.copy(dst, src)
-
-        cast_vals(0, 0)
-        cast_vals(0, 1)
-        p_all = sb.tile([P, PASSES, PACK, P], F32, name="p_all", tag="v_raw0_1", align_bytes=64)
-        p_tiles = []
+        for first, width in CHUNKS:
+            h, g0 = first // K_PASS, first % K_PASS // PAGE
+            pages = p[h][:].rearrange("q t (g j) -> q g t j", g=PAGES)[:, g0 : g0 + width // PAGE]
+            nc.vector.tensor_reduce(sums[h][:, g0 : g0 + width // PAGE], pages, AXIS.XY, ALU.add)
+        pf = []
         for h in range(PASSES):
-            p = p_all[:, h]
-            nc.scalar.activation(p, scores[h][:].rearrange("q (s t) -> q t s", t=PACK), ACT.Exp)
-            p_tiles.append(p)
-        nc.vector.tensor_reduce(neg_max[:], b[:], AXIS.X, ALU.max, negate=True)
-        nc.scalar.activation(r[:], b[:], ACT.Exp, bias=neg_max[:], accum_out=r_sum[:])
-
-        z_tiles, pf_tiles = [], []
-        for h in range(PASSES):
-            p = p_tiles[h]
-            z = sb.tile([P, PAGES], F32, name="z%d" % h)
-            nc.vector.tensor_reduce(z[:], p.rearrange("q t (g j) -> q g t j", j=PACK), AXIS.XY, ALU.add)
-            z_tiles.append(z)
-            p_turned = psum.tile([P, PACK, Q], F32, name="p_turned%d" % h, tag="bank%d" % (3 + h))
+            p_turned = psum.tile([P, PACK, Q], F32, name="p_turned%d" % h, offset=(2 + h) * BANK)
             for t in range(PACK):
-                nc.tensor.transpose(p_turned[:, t, :], p[:, t, :], ident[:])
-            pf = sb.tile([P, PACK, Q], F32, name="pf%d" % h, align_bytes=64)
+                nc.tensor.transpose(p_turned[:, t, :], p[h][:, t, :], ident[:])
+            pf.append(sb.tile([P, PACK, Q], F32, name="pf%d" % h, tag="pf%d" % h, align_bytes=ALIGN))
             for t in range(PACK):
-                nc.scalar.activation(pf[:, t, :], p_turned[:, t, :], ACT.Copy, scale=fac_t[:, h, t : t + 1])
-            pf_tiles.append(pf)
-        nc.vector.reciprocal(r_inv[:], r_sum[:])
-        z_invs = []
+                nc.scalar.activation(pf[h][:, t, :], p_turned[:, t, :], ACT.Copy, scale=fac_t[:, h, t : t + 1])
+
+        inverse = []
         for h in range(PASSES):
-            z_inv = sb.tile([P, PAGES], F32, name="z_inv%d" % h)
-            nc.vector.reciprocal(z_inv[:], z_tiles[h][:])
-            z_invs.append(z_inv)
-        shares = []
+            inverse.append(sb.tile([P, sum_width[h]], F32, name="inverse%d" % h, tag="inverse%d" % h, align_bytes=ALIGN))
+            nc.vector.reciprocal(inverse[h][:], sums[h][:])
+        share_turned = []
         for h in range(PASSES):
-            share = sb.tile([P, PAGES, PACK], F32, name="share%d" % h, align_bytes=64)
+            share = sb.tile([P, PAGES, PACK], F32, name="share%d" % h, align_bytes=ALIGN)
             nc.vector.scalar_tensor_tensor(
-                share[:], z_invs[h][:].unsqueeze(2).to_broadcast([P, PAGES, PACK]), r_inv[:],
-                r[:, h * PAGES : (h + 1) * PAGES].unsqueeze(2).to_broadcast([P, PAGES, PACK]), ALU.mult, ALU.mult,
-            )
-            share_turned = psum.tile([P, Q], F32, name="share_turned%d" % h, tag="bank%d" % (5 + h))
-            nc.tensor.transpose(share_turned[:], share[:].rearrange("q g j -> q (g j)"), ident[:])
-            shares.append(share_turned)
-        w_bfs = []
-        for h in range(PASSES):
-            w_bf = sb.tile([P, Q, PACK], BF16, name="w_bf%d" % h, align_bytes=64)
-            dst, src = interleave_views(w_bf[:], pf_tiles[h][:])
-            nc.vector.tensor_tensor(
-                dst, src,
-                shares[h][:].rearrange("s (c i) -> s c i", i=4).unsqueeze(2).to_broadcast([P, Q // 4, PACK, 4]),
+                share[:],
+                inverse[h][:, 0:PAGES].unsqueeze(2).to_broadcast([P, PAGES, PACK]),
+                inverse[0][:, PAGES : PAGES + 1],
+                r[:, h * PAGES : (h + 1) * PAGES].unsqueeze(2).to_broadcast([P, PAGES, PACK]),
+                ALU.mult,
                 ALU.mult,
             )
-            w_bfs.append(w_bf)
-        w_codes, w_planes = [], []
-        for h in range(PASSES):
-            w_codes.append(sb.tile([P, Q], U32, name="w_codes%d" % h, align_bytes=64))
-            w_planes.append(sb.tile([P, Q], U8, name="w_plane%d" % h, align_bytes=64))
-            nc.vector.quantize_mx(out=w_codes[h][:].bitcast(FP8X4), scales=w_planes[h][:], in_=w_bfs[h][:].rearrange("p q t -> p (q t)"))
+            share_turned.append(psum.tile([P, Q], F32, name="share_turned%d" % h, offset=(4 + h) * BANK))
+            nc.tensor.transpose(share_turned[h][:], share[:].rearrange("q g j -> q (g j)"), ident[:])
 
-        acc = [psum.tile([P, HALF], F32, name="acc%d" % u, tag="bank%d" % u) for u in range(2)]
+        quantise_values(0, 1, sb.tile([P, HALF], U32, name="codes0_1", tag="inverse0", align_bytes=ALIGN))
+        round_values(1, 0, "neg_max")
+        quantise_values(1, 0, sb.tile([P, HALF], U32, name="codes1_0", tag="inverse1", align_bytes=ALIGN))
+
+        w_bf = []
+        for h in range(PASSES):
+            w_bf.append(sb.tile([P, Q, PACK], BF16, name="w_bf%d" % h, align_bytes=ALIGN))
+            grouped, rows = interleave_views(w_bf[h][:], pf[h][:])
+            runs = share_turned[h][:].rearrange("s (c i) -> s c i", i=RUN)
+            nc.vector.tensor_tensor(grouped, rows, runs.unsqueeze(2).to_broadcast([P, Q // RUN, PACK, RUN]), ALU.mult)
+        weights = []
+        for h in range(PASSES):
+            w_codes = sb.tile([P, Q], U32, name="w_codes%d" % h, align_bytes=ALIGN)
+            w_plane = sb.tile([P, Q], U8, name="w_plane%d" % h, align_bytes=ALIGN)
+            quantise(nc, w_codes[:], w_plane[:], w_bf[h][:])
+            weights.append((w_codes[:], w_plane[:]))
+
+        round_values(1, 1, "fac_t")
+        quantise_values(1, 1, sb.tile([P, HALF], U32, name="codes1_1", tag="pf1", align_bytes=ALIGN))
+
+        acc = [psum.tile([P, HALF], F32, name="acc%d" % u, offset=(6 + u) * BANK) for u in range(2)]
         for h in range(PASSES):
             for u in range(2):
-                if (h, u) not in v_bfs:
-                    cast_vals(h, u)
-                v_bf = v_bfs[h, u]
-                v_codes = sb.tile([P, HALF], U32, name="v_codes%d_%d" % (h, u), align_bytes=64)
-                v_plane = sb.tile([P, HALF], U8, name="v_plane%d_%d" % (h, u), align_bytes=64)
-                nc.vector.quantize_mx(out=v_codes[:].bitcast(FP8X4), scales=v_plane[:], in_=v_bf[:].rearrange("p e t -> p (e t)"))
-                nc.tensor.matmul_mx(
-                    out=acc[u][:], lhsT=w_codes[h][:].bitcast(FP8X4), lhsT_scale=w_planes[h][:],
-                    rhs=v_codes[:].bitcast(FP8X4), rhs_scale=v_plane[:],
-                    start=(h == 0), stop=(h == PASSES - 1),
-                )
-
-        for u in range(2):
-            result = sb.tile([P, HALF], F32, name="result%d" % u)
-            if u == 0:
-                nc.scalar.copy(result[:], acc[u][:])
-                nc.scalar.dma_start(out[:, u * HALF : (u + 1) * HALF], result[:])
-            else:
-                nc.vector.tensor_copy(result[:], acc[u][:])
-                nc.sync.dma_start(out[:, u * HALF : (u + 1) * HALF], result[:])
+                product(nc, acc[u][:], weights[h], values[h, u], start=(h == 0), stop=(h == PASSES - 1))
+        result = [sb.tile([P, HALF], F32, name="result%d" % u) for u in range(2)]
+        nc.scalar.copy(result[0][:], acc[0][:])
+        nc.scalar.dma_start(out[:, 0:HALF], result[0][:])
+        nc.vector.tensor_copy(result[1][:], acc[1][:])
+        nc.sync.dma_start(out[:, HALF:E], result[1][:])

@@ -107,9 +107,9 @@ def tile_attend_landmark_kernel(tc, query, keys_words, keys_scales, marks_words,
         nc.sync.dma_start(q_raw[:], query.rearrange("(p t) q -> p t q", t=PACK))
         nc.sync.dma_start(key_pool[:], keys_words[0].rearrange("p n t -> p (n t)").bitcast(I32))
         load_values(0, 0)
-        load_values(0, 1)
         load_scale_rows(nc, mark_plane, marks_scales)
         nc.sync.dma_start(mark_pool[:], marks_words[0].rearrange("p n t -> p (n t)").bitcast(I32))
+        load_values(0, 1)
         load_values(1, 0)
         nc.sync.dma_start(fac_t[:], fac.rearrange("o (h p t) -> p (o h) t", p=P, t=PACK))
         load_values(1, 1)
@@ -142,8 +142,8 @@ def tile_attend_landmark_kernel(tc, query, keys_words, keys_scales, marks_words,
         v_bf = {}
         values = {}
 
-        def round_values(h, u, tag):
-            v_bf[h, u] = sb.tile([P, HALF, PACK], BF16, name="v_bf%d_%d" % (h, u), tag=tag, align_bytes=ALIGN)
+        def round_values(h, u, grouped):
+            v_bf[h, u] = grouped
             nc.scalar.copy(*interleave_views(v_bf[h, u][:], v_raw[h, u][:]))
 
         def quantise_values(h, u, codes):
@@ -151,7 +151,7 @@ def tile_attend_landmark_kernel(tc, query, keys_words, keys_scales, marks_words,
             quantise(nc, codes[:], plane[:], v_bf[h, u][:])
             values[h, u] = (codes[:], plane[:])
 
-        round_values(0, 0, "v_bf0_0")
+        round_values(0, 0, reused.tile([P, HALF, PACK], BF16, name="v_bf0_0", offset=marks_at + U * 4, align_bytes=ALIGN))
         quantise_values(0, 0, sb.tile([P, HALF], U32, name="codes0_0", align_bytes=ALIGN))
         v_bf[0, 1] = reused.tile([P, HALF, PACK], BF16, name="v_bf0_1", offset=marks_at + PASSES * sums_bytes, align_bytes=ALIGN)
         nc.gpsimd.tensor_scalar(v_bf[0, 1][:], v_raw[0, 1][:].rearrange("p t e -> p e t"), 1.0, 0.0, ALU.mult, ALU.add)
@@ -201,7 +201,7 @@ def tile_attend_landmark_kernel(tc, query, keys_words, keys_scales, marks_words,
             nc.tensor.transpose(share_turned[h][:], share[:].rearrange("q g j -> q (g j)"), ident[:])
 
         quantise_values(0, 1, sb.tile([P, HALF], U32, name="codes0_1", tag="inverse0", align_bytes=ALIGN))
-        round_values(1, 0, "neg_max")
+        round_values(1, 0, sb.tile([P, HALF, PACK], BF16, name="v_bf1_0", tag="neg_max", align_bytes=ALIGN))
         quantise_values(1, 0, sb.tile([P, HALF], U32, name="codes1_0", tag="inverse1", align_bytes=ALIGN))
 
         w_bf = []
@@ -217,7 +217,7 @@ def tile_attend_landmark_kernel(tc, query, keys_words, keys_scales, marks_words,
             quantise(nc, w_codes[:], w_plane[:], w_bf[h][:])
             weights.append((w_codes[:], w_plane[:]))
 
-        round_values(1, 1, "fac_t")
+        round_values(1, 1, sb.tile([P, HALF, PACK], BF16, name="v_bf1_1", tag="fac_t", align_bytes=ALIGN))
         quantise_values(1, 1, sb.tile([P, HALF], U32, name="codes1_1", tag="pf1", align_bytes=ALIGN))
 
         acc = [psum.tile([P, HALF], F32, name="acc%d" % u, offset=(6 + u) * BANK) for u in range(2)]

from contextlib import ExitStack

import concourse.mybir as mybir
from concourse.masks import make_identity

D, T, U, I, G, Q, E = 512, 2048, 512, 1024, 64, 128, 512
FLOPS = 2 * D * Q * (I + G) + 2 * I * Q * E

F32 = mybir.dt.float32
BF16 = mybir.dt.bfloat16
I32 = mybir.dt.int32
U32 = mybir.dt.uint32
U16 = mybir.dt.uint16
U8 = mybir.dt.uint8
FP8X4 = mybir.dt.float8_e4m3fn_x4
ALU = mybir.AluOpType
ACT = mybir.ActivationFunctionType
AXIS = mybir.AxisListType

P = 128
PACK = 4
K_PASS = P * PACK
PASSES = I // K_PASS
PAGE = I // G
PAGES = G // PASSES
LIST_ROWS = 16
HALF = E // 2
RUN = 4
BANK = 2048
CHUNKS = [(0, K_PASS), (K_PASS, K_PASS // 2), (K_PASS + K_PASS // 2, K_PASS // 2)]
SCORE_BANKS = [0, 1, 6]
ALIGN = 64


def load_scale_rows(nc, plane, rows):
    for n in range(4):
        nc.sync.dma_start(plane[32 * n : 32 * n + 4, :].bitcast(I32), rows[0, 4 * n : 4 * n + 4, :].bitcast(I32))


def interleave_views(grouped, rows):
    return (
        grouped.rearrange("p (c i) t -> p c t i", i=RUN),
        rows.rearrange("p t (c i) -> p c t i", i=RUN),
    )


def quantise(nc, codes, plane, grouped):
    nc.vector.quantize_mx(out=codes.bitcast(FP8X4), scales=plane, in_=grouped.rearrange("p c t -> p (c t)"))


def product(nc, out, stationary, moving, start=True, stop=True):
    nc.tensor.matmul_mx(
        out=out,
        lhsT=stationary[0].bitcast(FP8X4),
        lhsT_scale=stationary[1],
        rhs=moving[0].bitcast(FP8X4),
        rhs_scale=moving[1],
        start=start,
        stop=stop,
    )


def tile_attend_landmark_kernel(tc, query, keys_words, keys_scales, marks_words, marks_scales, fac, vals, offs, offs2, out):
    nc = tc.nc
    with ExitStack() as ctx:
        lists = ctx.enter_context(tc.tile_pool(name="lists", bufs=1))
        sb = ctx.enter_context(tc.tile_pool(name="sb", bufs=1))
        reused = ctx.enter_context(tc.tile_pool(name="reused", bufs=1))
        psum = ctx.enter_context(tc.psum_pool(name="psum", bufs=1))

        p_bytes = K_PASS * 4
        marks_at = PASSES * p_bytes
        sums_bytes = 3 * ALIGN

        key_list = lists.tile([P, I // LIST_ROWS], U16, name="key_list")
        mark_list = lists.tile([P, G // LIST_ROWS], U16, name="mark_list")
        key_plane = sb.tile([P, T], U8, name="key_plane", align_bytes=ALIGN)
        mark_plane = sb.tile([P, U], U8, name="mark_plane", align_bytes=ALIGN)
        key_pool = sb.tile([P, T], I32, name="key_pool", align_bytes=ALIGN)
        mark_pool = reused.tile([P, U], I32, name="mark_pool", offset=marks_at, align_bytes=ALIGN)
        q_raw = sb.tile([P, PACK, Q], F32, name="q_raw", align_bytes=ALIGN)
        fac_t = sb.tile([P, PASSES, PACK], F32, name="fac_t", tag="fac_t", align_bytes=ALIGN)
        ident = sb.tile([P, P], F32, name="ident", align_bytes=ALIGN)

        nc.gpsimd.memset(key_plane[:].bitcast(I32), 0)
        nc.gpsimd.memset(mark_plane[:].bitcast(I32), 0)
        warm_in = sb.tile([P, 1], F32, name="warm_in")
        warm_out = sb.tile([P, 1], F32, name="warm_out")
        nc.gpsimd.memset(warm_in[:], 0.0)
        nc.scalar.activation(warm_out[:], warm_in[:], ACT.Exp)
        make_identity(nc, ident[:])

        v_rows = vals.rearrange("(h p t) e -> h p t e", p=P, t=PACK)
        v_raw = {
            (0, 0): reused.tile([P, PACK, HALF], F32, name="v_raw0_0", offset=0, align_bytes=ALIGN),
            (0, 1): sb.tile([P, PACK, HALF], F32, name="v_raw0_1", align_bytes=ALIGN),
            (1, 0): sb.tile([P, PACK, HALF], F32, name="v_raw1_0", align_bytes=ALIGN),
            (1, 1): sb.tile([P, PACK, HALF], F32, name="v_raw1_1", align_bytes=ALIGN),
        }

        def load_values(h, u):
            nc.sync.dma_start(v_raw[h, u][:], v_rows[h][:, :, u * HALF : (u + 1) * HALF])

        load_scale_rows(nc, key_plane, keys_scales)
        nc.sync.dma_start(key_list[:], offs)
        nc.sync.dma_start(mark_list[:], offs2)
        nc.sync.dma_start(q_raw[:], query.rearrange("(p t) q -> p t q", t=PACK))
        nc.sync.dma_start(key_pool[:], keys_words[0].rearrange("p n t -> p (n t)").bitcast(I32))
        load_values(0, 0)
        load_scale_rows(nc, mark_plane, marks_scales)
        nc.sync.dma_start(mark_pool[:], marks_words[0].rearrange("p n t -> p (n t)").bitcast(I32))
        load_values(0, 1)
        load_values(1, 0)
        nc.sync.dma_start(fac_t[:], fac.rearrange("o (h p t) -> p (o h) t", p=P, t=PACK))
        load_values(1, 1)

        q_bf = sb.tile([P, Q, PACK], BF16, name="q_bf", align_bytes=ALIGN)
        q_codes = sb.tile([P, Q], U32, name="q_codes", align_bytes=ALIGN)
        q_plane = sb.tile([P, Q], U8, name="q_plane", align_bytes=ALIGN)
        nc.scalar.copy(*interleave_views(q_bf[:], q_raw[:]))
        k_plane = sb.tile([P, I], U8, name="k_plane", align_bytes=ALIGN)
        nc.vector.tensor_copy(k_plane[:], key_plane[:].indirect(key_list[:]))
        quantise(nc, q_codes[:], q_plane[:], q_bf[:])
        queries = (q_codes[:], q_plane[:])
        scores = []
        for n, (first, width) in enumerate(CHUNKS):
            entries = key_list[:, first // LIST_ROWS : (first + width) // LIST_ROWS]
            k_codes = sb.tile([P, width], U32, name="k_codes%d" % n, align_bytes=ALIGN)
            nc.vector.tensor_copy(k_codes[:], key_pool[:].bitcast(U32).indirect(entries))
            scores.append(psum.tile([P, width], F32, name="scores%d" % n, offset=SCORE_BANKS[n] * BANK))
            product(nc, scores[n][:], queries, (k_codes[:], k_plane[:, first : first + width]))

        m_plane = sb.tile([P, G], U8, name="m_plane", align_bytes=ALIGN)
        m_codes = sb.tile([P, G], U32, name="m_codes", align_bytes=ALIGN)
        nc.vector.tensor_copy(m_plane[:], mark_plane[:].indirect(mark_list[:]))
        nc.vector.tensor_copy(m_codes[:], mark_pool[:].bitcast(U32).indirect(mark_list[:]))
        mark_banks = psum.tile([P, PASSES * K_PASS], F32, name="mark_banks", offset=2 * BANK)
        mark_scores = mark_banks[:, 0:G]
        product(nc, mark_scores, queries, (m_codes[:], m_plane[:]))

        neg_max = sb.tile([P, 1], F32, name="neg_max", tag="neg_max", align_bytes=ALIGN)
        v_bf = {}
        values = {}

        def round_values(h, u, grouped):
            v_bf[h, u] = grouped
            nc.scalar.copy(*interleave_views(v_bf[h, u][:], v_raw[h, u][:]))

        def quantise_values(h, u, codes):
            plane = sb.tile([P, HALF], U8, name="v_plane%d_%d" % (h, u), align_bytes=ALIGN)
            quantise(nc, codes[:], plane[:], v_bf[h, u][:])
            values[h, u] = (codes[:], plane[:])

        round_values(0, 0, reused.tile([P, HALF, PACK], BF16, name="v_bf0_0", offset=marks_at + U * 4, align_bytes=ALIGN))
        quantise_values(0, 0, sb.tile([P, HALF], U32, name="codes0_0", align_bytes=ALIGN))
        v_bf[0, 1] = reused.tile([P, HALF, PACK], BF16, name="v_bf0_1", offset=marks_at + PASSES * sums_bytes, align_bytes=ALIGN)
        nc.gpsimd.tensor_scalar(v_bf[0, 1][:], v_raw[0, 1][:].rearrange("p t e -> p e t"), 1.0, 0.0, ALU.mult, ALU.add)

        p = [reused.tile([P, PACK, P], F32, name="p%d" % h, offset=h * p_bytes, align_bytes=ALIGN) for h in range(PASSES)]
        for n, (first, width) in enumerate(CHUNKS):
            h, s0 = first // K_PASS, first % K_PASS // PACK
            nc.scalar.activation(p[h][:, :, s0 : s0 + width // PACK], scores[n][:].rearrange("q (s t) -> q t s", t=PACK), ACT.Exp)
        sum_width = [PAGES + 1, PAGES]
        sums = [
            reused.tile([P, sum_width[h]], F32, name="sums%d" % h, offset=marks_at + h * sums_bytes, align_bytes=ALIGN)
            for h in range(PASSES)
        ]
        r = sb.tile([P, G], F32, name="r")
        nc.vector.tensor_reduce(neg_max[:], mark_scores, AXIS.X, ALU.max, negate=True)
        nc.scalar.activation(r[:], mark_scores, ACT.Exp, bias=neg_max[:], accum_out=sums[0][:, PAGES : PAGES + 1])

        for first, width in CHUNKS:
            h, g0 = first // K_PASS, first % K_PASS // PAGE
            pages = p[h][:].rearrange("q t (g j) -> q g t j", g=PAGES)[:, g0 : g0 + width // PAGE]
            nc.vector.tensor_reduce(sums[h][:, g0 : g0 + width // PAGE], pages, AXIS.XY, ALU.add)
        pf = []
        for h in range(PASSES):
            p_turned = psum.tile([P, PACK, Q], F32, name="p_turned%d" % h, offset=(2 + h) * BANK)
            for t in range(PACK):
                nc.tensor.transpose(p_turned[:, t, :], p[h][:, t, :], ident[:])
            pf.append(sb.tile([P, PACK, Q], F32, name="pf%d" % h, tag="pf%d" % h, align_bytes=ALIGN))
            for t in range(PACK):
                nc.scalar.activation(pf[h][:, t, :], p_turned[:, t, :], ACT.Copy, scale=fac_t[:, h, t : t + 1])

        inverse = []
        for h in range(PASSES):
            inverse.append(sb.tile([P, sum_width[h]], F32, name="inverse%d" % h, tag="inverse%d" % h, align_bytes=ALIGN))
            nc.vector.reciprocal(inverse[h][:], sums[h][:])
        share_turned = []
        for h in range(PASSES):
            share = sb.tile([P, PAGES, PACK], F32, name="share%d" % h, align_bytes=ALIGN)
            nc.vector.scalar_tensor_tensor(
                share[:],
                inverse[h][:, 0:PAGES].unsqueeze(2).to_broadcast([P, PAGES, PACK]),
                inverse[0][:, PAGES : PAGES + 1],
                r[:, h * PAGES : (h + 1) * PAGES].unsqueeze(2).to_broadcast([P, PAGES, PACK]),
                ALU.mult,
                ALU.mult,
            )
            share_turned.append(psum.tile([P, Q], F32, name="share_turned%d" % h, offset=(4 + h) * BANK))
            nc.tensor.transpose(share_turned[h][:], share[:].rearrange("q g j -> q (g j)"), ident[:])

        quantise_values(0, 1, sb.tile([P, HALF], U32, name="codes0_1", tag="inverse0", align_bytes=ALIGN))
        round_values(1, 0, sb.tile([P, HALF, PACK], BF16, name="v_bf1_0", tag="neg_max", align_bytes=ALIGN))
        quantise_values(1, 0, sb.tile([P, HALF], U32, name="codes1_0", tag="inverse1", align_bytes=ALIGN))

        w_bf = []
        for h in range(PASSES):
            w_bf.append(sb.tile([P, Q, PACK], BF16, name="w_bf%d" % h, align_bytes=ALIGN))
            grouped, rows = interleave_views(w_bf[h][:], pf[h][:])
            runs = share_turned[h][:].rearrange("s (c i) -> s c i", i=RUN)
            nc.vector.tensor_tensor(grouped, rows, runs.unsqueeze(2).to_broadcast([P, Q // RUN, PACK, RUN]), ALU.mult)
        weights = []
        for h in range(PASSES):
            w_codes = sb.tile([P, Q], U32, name="w_codes%d" % h, align_bytes=ALIGN)
            w_plane = sb.tile([P, Q], U8, name="w_plane%d" % h, align_bytes=ALIGN)
            quantise(nc, w_codes[:], w_plane[:], w_bf[h][:])
            weights.append((w_codes[:], w_plane[:]))

        round_values(1, 1, sb.tile([P, HALF, PACK], BF16, name="v_bf1_1", tag="fac_t", align_bytes=ALIGN))
        quantise_values(1, 1, sb.tile([P, HALF], U32, name="codes1_1", tag="pf1", align_bytes=ALIGN))

        acc = [psum.tile([P, HALF], F32, name="acc%d" % u, offset=(6 + u) * BANK) for u in range(2)]
        for h in range(PASSES):
            for u in range(2):
                product(nc, acc[u][:], weights[h], values[h, u], start=(h == 0), stop=(h == PASSES - 1))
        result = [sb.tile([P, HALF], F32, name="result%d" % u) for u in range(2)]
        nc.scalar.copy(result[0][:], acc[0][:])
        nc.scalar.dma_start(out[:, 0:HALF], result[0][:])
        nc.vector.tensor_copy(result[1][:], acc[1][:])
        nc.sync.dma_start(out[:, HALF:E], result[1][:])
